import numpy as np
import ml_dtypes


def mxq(x, axis, fmt="e4m3"):
    dtype, down = {"e4m3": (ml_dtypes.float8_e4m3fn, 7), "e5m2": (ml_dtypes.float8_e5m2, 14)}[fmt]
    v = np.moveaxis(np.asarray(x, np.float32).astype(ml_dtypes.bfloat16).astype(np.float64), axis, -1)
    blocks = v.reshape(v.shape[:-1] + (-1, 32))
    amax = np.abs(blocks).max(-1, keepdims=True)
    byte = np.maximum(np.where(amax > 0, np.frexp(amax)[1] - 1 + 127, 0) - down, 1)
    scale = np.exp2(byte - 127.0)
    codes = (blocks / scale).astype(np.float32).astype(dtype).astype(np.float64)
    return np.moveaxis((codes * scale).reshape(v.shape), -1, axis)


WIDE = False


def mx_kscale(k):
    if not WIDE:
        return np.ones(k)
    levels = np.array([10, -10, 5, -5, 0])
    if k % 512:
        return np.exp2(np.random.permutation(np.resize(levels, k // 32))).repeat(32)
    a = np.empty((k // 512, 16))
    for p in range(k // 512):
        a[p, :8] = np.random.permutation(np.resize(levels, 8))
        for g in range(8):
            far = levels[np.abs(levels - a[p, g]) >= 10]
            a[p, g + 8] = far[np.random.randint(len(far))]
    return np.exp2(a.ravel()).repeat(32)


BF16 = ml_dtypes.bfloat16


def bf(x):
    return np.asarray(x, np.float32).astype(BF16)


def f64(x):
    return np.asarray(x).astype(np.float64)


E2M1 = np.array([0.0, 0.5, 1.0, 1.5, 2.0, 3.0, 4.0, 6.0, -0.0, -0.5, -1.0, -1.5, -2.0, -3.0, -4.0, -6.0])


def pack_weight(w, fmt):
    k, n = w.shape
    w = f64(bf(w)).reshape(k // 32, 32, n)
    amax = np.abs(w).max(1)
    if fmt == "e4m3":
        byte = np.frexp(amax)[1] - 1 + 127 - 7
    else:
        mant, ex = np.frexp(amax / 6.0)
        byte = np.where(mant > 0.5, ex, ex - 1) + 127
    byte = np.clip(np.where(amax > 0, byte, 1), 1, 254)
    scaled = (w * np.exp2(127.0 - byte)[:, None, :]).reshape(k, n).astype(np.float32)
    by_word = np.ascontiguousarray(scaled.reshape(k // 512, 128, 4, n).transpose(0, 1, 3, 2))
    if fmt == "e4m3":
        words = by_word.astype(ml_dtypes.float8_e4m3fn).view(np.uint8)
    else:
        c = by_word.astype(ml_dtypes.float4_e2m1fn).view(np.uint8) & 0xF
        words = c[..., 0::2] | (c[..., 1::2] << 4)
    return np.ascontiguousarray(words), np.ascontiguousarray(byte.astype(np.uint8).reshape(k // 512, 16, n))


def unpack_weight(words, scales, fmt):
    g, p, n, _ = words.shape
    if fmt == "e4m3":
        vals = np.ascontiguousarray(words).view(ml_dtypes.float8_e4m3fn).astype(np.float64)
    else:
        nib = np.empty((g, p, n, 4), np.uint8)
        nib[..., 0::2] = words & 0xF
        nib[..., 1::2] = words >> 4
        vals = E2M1[nib]
    vals = vals * np.repeat(np.exp2(scales.astype(np.float64) - 127.0), 8, axis=1)[..., None]
    return vals.transpose(0, 1, 3, 2).reshape(g * 512, n)
def pack4(w):
    words, scales = pack_weight(w, "e2m1")
    return words.reshape(words.shape[0], 128, -1), scales


def unpack4(words, scales):
    return unpack_weight(words.reshape(words.shape[0], 128, -1, 2), scales, "e2m1")


def planes(Y):
    n, m = Y.shape
    b = f64(bf(Y)).reshape(n // 32, 32, m)
    amax = np.abs(b).max(1)
    byte = np.clip(np.where(amax > 0, np.frexp(amax)[1] - 1 + 127 - 7, 1), 1, 254)
    codes = (b * np.exp2(127.0 - byte)[:, None, :]).reshape(n, m).astype(np.float32).astype(ml_dtypes.float8_e4m3fn).view(np.uint8)
    words = codes.reshape(n // 512, 128, 4, m).transpose(0, 1, 3, 2)
    return np.ascontiguousarray(words), np.ascontiguousarray(byte.astype(np.uint8).reshape(n // 512, 16, m))


N, M, K, R = 2048, 1024, 1536, 512


def setup_inputs():
    s_n, s_k, s_r = mx_kscale(N), mx_kscale(K), mx_kscale(R)
    spread = np.exp(0.7 * np.random.randn(N))
    b = bf(np.random.randn(N, M) * s_n[:, None])
    e = bf(spread / s_n)
    left = bf(np.random.randn(N, R) / np.sqrt(N) / R ** 0.25 / s_n[:, None] / s_r)
    z = bf(np.random.randn(K, N) * spread * s_k[:, None])
    h = bf(np.random.randn(K, R) / np.sqrt(K) / R ** 0.25 / s_k[:, None] * s_r)
    theta = bf(0.5 + np.random.rand(R))
    z_words, z_scales = pack_weight(f64(z), "e4m3")
    l_words, l_scales = pack4(f64(left))
    return {"z_words": z_words, "z_scales": z_scales, "h": h, "l_words": l_words,
            "l_scales": l_scales, "b": b, "theta": theta, "e": e}

def reference(z_words, z_scales, h, l_words, l_scales, b, theta, e):
    Z = unpack_weight(z_words, z_scales, "e4m3")
    L = unpack4(l_words, l_scales)
    H, B, th, ev = f64(h), f64(b), f64(theta), f64(e)
    V = Z.T @ mxq(H, 0, "e4m3")
    C = th[:, None] * (L.T @ mxq(B, 0, "e4m3"))
    D = mxq(V, 1, "e4m3") @ mxq(C, 0, "e4m3")
    y = ev[:, None] * B - D
    Y = y.reshape(N, M)
    words, scales = planes(Y)
    return y, words, scales

@@ -1,0 +1,419 @@
+from contextlib import ExitStack
+
+import concourse.mybir as mybir
+
+N, M, K, R = 2048, 1024, 1536, 512
+FLOPS = 2 * K * N * R + 2 * N * R * M + 2 * R * N * M
+
+F32 = mybir.dt.float32
+BF16 = mybir.dt.bfloat16
+I32 = mybir.dt.int32
+U32 = mybir.dt.uint32
+U8 = mybir.dt.uint8
+FP8X4 = mybir.dt.float8_e4m3fn_x4
+FP4X4 = mybir.dt.float4_e2m1fn_x4
+COPY = mybir.ActivationFunctionType.Copy
+ALU = mybir.AluOpType
+
+P = 128
+PACK = 4
+W = 512
+GROUPS = N // W
+HALVES = M // W
+K_PASSES = K // W
+QUADRANTS = 4
+BANKS = 8
+CHUNK = 128
+Y_GROUPED_BUFS = 1
+LAG = 1
+
+
+def tile_oblique_block_deflation_k4_kernel(
+    tc, z_words, z_scales, h, l_words, l_scales, b, theta, e, out_0, out_1, out_2
+):
+    nc = tc.nc
+    with ExitStack() as ctx:
+        keep = ctx.enter_context(tc.tile_pool(name="keep", bufs=1))
+        stage = ctx.enter_context(tc.tile_pool(name="stage", bufs=1))
+        psum = ctx.enter_context(tc.psum_pool(name="psum", bufs=1))
+        ctx.enter_context(tc.manual_schedule())
+
+        def kept(name, shape, dtype):
+            return keep.tile(shape, dtype, name=name, align_bytes=64)
+
+        def staged(tag, shape, dtype, bufs):
+            return stage.tile(shape, dtype, name=tag, tag=tag, bufs=bufs, align_bytes=64)
+
+        free_banks = list(range(BANKS))
+        banks = {}
+        bank_number = {}
+
+        def take_bank(key):
+            bank_number[key] = free_banks.pop(0)
+            tag = "bank%d" % bank_number[key]
+            banks[key] = psum.tile([P, W], F32, name=tag, tag=tag)
+            return banks[key]
+
+        def give_bank(key):
+            free_banks.append(bank_number[key])
+
+        on_vector = nc.vector.tensor_copy
+        on_scalar = nc.scalar.copy
+
+        def on_scalar_by_activation(out, in_):
+            nc.scalar.activation(out=out, in_=in_, func=COPY)
+
+        def on_gpsimd(out, in_):
+            nc.gpsimd.tensor_scalar(out=out, in0=in_, scalar1=1.0, scalar2=0.0, op0=ALU.mult, op1=ALU.add)
+
+        units = [(g, half) for g in range(GROUPS) for half in range(HALVES)]
+        b_raw = {}
+        b_codes = {u: kept("b_codes%d%d" % u, [P, W], U32) for u in units}
+        b_planes = {u: kept("b_planes%d%d" % u, [P, W], U8) for u in units}
+        y_codes = {}
+        h_raw = [kept("h_raw%d" % k, [P, PACK, R], BF16) for k in range(K_PASSES)]
+        h_codes = [kept("h_codes%d" % k, [P, R], U32) for k in range(K_PASSES)]
+        h_planes = [kept("h_planes%d" % k, [P, R], U8) for k in range(K_PASSES)]
+        z_codes = [kept("z_codes%d" % g, [P, K_PASSES, W], U32) for g in range(GROUPS)]
+        z_planes = kept("z_planes", [P, N], U8)
+        l_raw = kept("l_raw", [P, GROUPS, 2 * R], U8)
+        l_codes = kept("l_codes", [P, GROUPS, 2 * R], U8)
+        l_planes_raw = kept("l_planes_raw", [P, GROUPS, R], U8)
+        l_planes = kept("l_planes", [P, GROUPS, R], U8)
+        v_codes = [kept("v_codes%d" % g, [P, W], U32) for g in range(GROUPS)]
+        v_planes = [kept("v_planes%d" % g, [P, W], U8) for g in range(GROUPS)]
+        c_codes = [kept("c_codes%d" % half, [P, W], U32) for half in range(HALVES)]
+        c_planes = [kept("c_planes%d" % half, [P, W], U8) for half in range(HALVES)]
+        c_rows = [kept("c_rows%d" % half, [P, PACK, W], BF16) for half in range(HALVES)]
+        y_planes = kept("y_planes", [P, M], U8)
+        theta_raw = kept("theta_raw", [P, PACK], BF16)
+        theta_f32 = kept("theta_f32", [P, PACK], F32)
+        e_cols = kept("e_cols", [P, GROUPS, PACK], BF16)
+
+        grouped = {}
+        y_rows = {}
+
+        def cols(half):
+            return slice(half * W, (half + 1) * W)
+
+        def rows(g):
+            return slice(g * W, (g + 1) * W)
+
+        def clear_planes():
+            nc.vector.memset(l_planes_raw[:].rearrange("p g r -> p (g r)").bitcast(I32), 0)
+            nc.vector.memset(z_planes[:].bitcast(I32), 0)
+
+        def load_b(g, half):
+            tile = kept("b_raw%d%d" % (g, half), [P, PACK, W], BF16)
+            b_raw[g, half] = tile[:]
+            nc.sync.dma_start(out=tile[:], in_=b[rows(g), cols(half)].rearrange("(p t) m -> p t m", t=PACK))
+
+        def load_b_rows(g):
+            tile = kept("b_rows%d" % g, [P, PACK, M], BF16)
+            for half in range(HALVES):
+                b_raw[g, half] = tile[:, :, cols(half)]
+            nc.sync.dma_start(out=tile[:], in_=b[rows(g), :].rearrange("(p t) m -> p t m", t=PACK))
+
+        def load_h(k):
+            nc.sync.dma_start(out=h_raw[k][:], in_=h[rows(k), :].rearrange("(p t) r -> p t r", t=PACK))
+
+        def load_l():
+            nc.sync.dma_start(
+                out=l_raw[:].bitcast(I32), in_=l_words.rearrange("g p n -> p g n").bitcast(I32)
+            )
+
+        def load_z(g):
+            flat = z_words.rearrange("k p n t -> p k (n t)")
+            nc.sync.dma_start(
+                out=z_codes[g][:].bitcast(I32),
+                in_=flat[:, :, PACK * W * g : PACK * W * (g + 1)].bitcast(I32),
+            )
+
+        def load_l_scales():
+            for q in range(QUADRANTS):
+                nc.sync.dma_start(
+                    out=l_planes_raw[32 * q : 32 * q + 4, :, :].bitcast(I32),
+                    in_=l_scales[:, 4 * q : 4 * q + 4, :].rearrange("g r n -> r g n").bitcast(I32),
+                )
+
+        def load_z_scales():
+            for q in range(QUADRANTS):
+                nc.sync.dma_start(
+                    out=z_planes[32 * q : 32 * q + 4 * K_PASSES, :].bitcast(I32),
+                    in_=z_scales[:, 4 * q : 4 * q + 4, :].bitcast(I32),
+                )
+
+        def load_theta():
+            with nc.allow_non_contiguous_dma(reason="one theta value a slot"):
+                for i in range(4):
+                    nc.gpsimd.dma_start(
+                        out=theta_raw[i:P:4, :],
+                        in_=theta.rearrange("(a t i) -> i a t", t=PACK, i=4)[i],
+                    )
+
+        def load_e():
+            nc.gpsimd.dma_start(out=e_cols[:], in_=e.rearrange("(g p t) -> p g t", p=P, t=PACK))
+
+        def widen_theta():
+            nc.vector.tensor_copy(out=theta_f32[:], in_=theta_raw[:])
+
+        def grouped_tile(key, tag, bufs):
+            if key not in grouped:
+                grouped[key] = staged(tag, [P, W, PACK], BF16, bufs)
+            return grouped[key]
+
+        def interleave(copy, dst, src, lo, hi):
+            copy(
+                out=dst[:, lo:hi, :].rearrange("p (c i) t -> p c t i", i=4),
+                in_=src[:, :, lo:hi].rearrange("p t (c i) -> p c t i", i=4),
+            )
+
+        def quantise(key, codes, plane):
+            nc.vector.quantize_mx(
+                out=codes[:].bitcast(FP8X4), scales=plane, in_=grouped[key][:].rearrange("p w t -> p (w t)")
+            )
+
+        def interleave_b(g, half, lo, hi, copy):
+            interleave(copy, grouped_tile(("b", g, half), "grouped_in", 4), b_raw[g, half], lo, hi)
+
+        def quantise_b(g, half):
+            quantise(("b", g, half), b_codes[g, half], b_planes[g, half][:])
+
+        def interleave_h(k, lo, hi, copy):
+            dst = grouped_tile(("h", k), "grouped_in", 4)
+            copy(
+                out=dst[:].rearrange("p (t a i) j -> p a t j i", t=PACK, i=4)[:, :, lo:hi],
+                in_=h_raw[k][:].rearrange("p j (a t i) -> p a t j i", t=PACK, i=4)[:, :, lo:hi],
+            )
+
+        def quantise_h(k):
+            quantise(("h", k), h_codes[k], h_planes[k][:])
+
+        def permute_l():
+            nc.vector.tensor_copy(
+                out=l_codes[:].bitcast(I32).rearrange("p g (t a w) -> p g t a w", t=PACK, w=2),
+                in_=l_raw[:].bitcast(I32).rearrange("p g (a t w) -> p g t a w", t=PACK, w=2),
+            )
+            nc.vector.tensor_copy(
+                out=l_planes[:].bitcast(I32).rearrange("p g (t a) -> p g t a", t=PACK),
+                in_=l_planes_raw[:].bitcast(I32).rearrange("p g (a t) -> p g t a", t=PACK),
+            )
+
+        def c_pass(half, t, g):
+            if g == 0:
+                take_bank(("c", half, t))
+            nc.tensor.matmul_mx(
+                out=banks["c", half, t][:],
+                lhsT=l_codes[:, g, 2 * P * t : 2 * P * (t + 1)].bitcast(FP4X4),
+                lhsT_scale=l_planes[:, g, P * t : P * (t + 1)],
+                rhs=b_codes[g, half][:].bitcast(FP8X4),
+                rhs_scale=b_planes[g, half][:],
+                start=(g == 0),
+                stop=(g == GROUPS - 1),
+            )
+
+        def c_out(half, t, copy):
+            if copy is on_vector:
+                nc.vector.tensor_scalar(
+                    out=c_rows[half][:, t, :], in0=banks["c", half, t][:], scalar1=theta_f32[:, t : t + 1],
+                    scalar2=None, op0=ALU.mult,
+                )
+            else:
+                nc.scalar.activation(
+                    out=c_rows[half][:, t, :], in_=banks["c", half, t][:], func=COPY, scale=theta_f32[:, t : t + 1]
+                )
+            give_bank(("c", half, t))
+
+        def interleave_c(half, lo, hi, copy):
+            interleave(copy, grouped_tile(("c", half), "grouped_c", 2), c_rows[half], lo, hi)
+
+        def quantise_c(half):
+            quantise(("c", half), c_codes[half], c_planes[half][:])
+
+        def v_passes(g, c):
+            bank = take_bank(("v", g, c))
+            for t in range(PACK):
+                for k in range(K_PASSES):
+                    nc.tensor.matmul_mx(
+                        out=bank[:, CHUNK * t : CHUNK * (t + 1)],
+                        lhsT=h_codes[k][:, P * t : P * (t + 1)].bitcast(FP8X4),
+                        lhsT_scale=h_planes[k][:, P * t : P * (t + 1)],
+                        rhs=z_codes[g][:, k, CHUNK * c : CHUNK * (c + 1)].bitcast(FP8X4),
+                        rhs_scale=z_planes[4 * k : P, W * g + CHUNK * c : W * g + CHUNK * (c + 1)],
+                        start=(k == 0),
+                        stop=(k == K_PASSES - 1),
+                    )
+
+        def v_out(g, c, copy):
+            dst = grouped_tile(("v", g), "grouped_v", 2)
+            copy(
+                out=dst[:].rearrange("p (s m) t -> p s m t", s=PACK)[:, :, 32 * c : 32 * (c + 1), :],
+                in_=banks["v", g, c][:].rearrange("p (t m s) -> p s m t", t=PACK, s=PACK),
+            )
+            give_bank(("v", g, c))
+
+        def quantise_v(g):
+            quantise(("v", g), v_codes[g], v_planes[g][:])
+
+        def d_pass(g, half, s):
+            take_bank(("d", g, half, s))
+            nc.tensor.matmul_mx(
+                out=banks["d", g, half, s][:],
+                lhsT=v_codes[g][:, P * s : P * (s + 1)].bitcast(FP8X4),
+                lhsT_scale=v_planes[g][:, P * s : P * (s + 1)],
+                rhs=c_codes[half][:].bitcast(FP8X4),
+                rhs_scale=c_planes[half][:],
+                start=True,
+                stop=True,
+            )
+
+        def y_out(g, half, s):
+            if s == 0:
+                y_rows[g, half] = staged("y_rows", [P, PACK, W], F32, 5)
+            nc.vector.scalar_tensor_tensor(
+                out=y_rows[g, half][:, s, :],
+                in0=b_raw[g, half][:, s, :],
+                scalar=e_cols[:, g, s : s + 1],
+                in1=banks["d", g, half, s][:],
+                op0=ALU.mult,
+                op1=ALU.subtract,
+            )
+            give_bank(("d", g, half, s))
+
+        def interleave_y(g, half, lo, hi, copy):
+            interleave(copy, grouped_tile(("y", g, half), "grouped_y", Y_GROUPED_BUFS), y_rows[g, half], lo, hi)
+
+        def quantise_y(g, half):
+            y_codes[g, half] = staged("y_codes", [P, W], U32, 4)
+            quantise(("y", g, half), y_codes[g, half], y_planes[4 * g : P, cols(half)])
+
+        def store_y(g, half, lo, hi):
+            nc.sync.dma_start(
+                out=out_0[rows(g), cols(half)].rearrange("(p s) m -> p s m", s=PACK)[:, lo:hi, :],
+                in_=y_rows[g, half][:, lo:hi, :],
+            )
+
+        def store_codes(g, half):
+            flat = out_1[g].rearrange("p m t -> p (m t)")
+            nc.sync.dma_start(
+                out=flat[:, PACK * W * half : PACK * W * (half + 1)].bitcast(I32),
+                in_=y_codes[g, half][:].bitcast(I32),
+            )
+
+        def store_scales():
+            for q in range(QUADRANTS):
+                nc.scalar.dma_start(
+                    out=out_2[:, 4 * q : 4 * q + 4, :].bitcast(I32),
+                    in_=y_planes[32 * q : 32 * q + 4 * GROUPS, :].bitcast(I32),
+                )
+
+        clear_planes()
+        load_theta()
+        load_e()
+        load_b(0, 0)
+        load_b(0, 1)
+        load_b(1, 0)
+        load_l_scales()
+        load_l()
+        load_b(1, 1)
+        for u in [(2, 0), (2, 1), (3, 0), (3, 1)]:
+            load_b(*u)
+        load_h(0)
+        load_z_scales()
+        load_h(1)
+        load_h(2)
+        for g in range(GROUPS):
+            load_z(g)
+
+        MID = W // 2
+        def c_passes(half, g):
+            for t in range(PACK):
+                c_pass(half, t, g)
+        def d_passes(g, half):
+            for s in range(PACK):
+                d_pass(g, half, s)
+        def shared(step, *key, cut=MID, end=W):
+            step(*key, 0, cut, on_vector)
+            if cut < end:
+                step(*key, cut, end, on_scalar)
+        order = [(g, half) for g in range(GROUPS) for half in range(HALVES)]
+
+        CUT = 240
+        for i, (g, half) in enumerate(order):
+            interleave_b(g, half, 0, CUT, on_vector)
+            interleave_b(g, half, CUT, W, on_scalar_by_activation if i == 0 else on_scalar)
+            if i > 0:
+                quantise_b(*order[i - 1])
+            if i == 2:
+                permute_l()
+                c_passes(0, 0)
+            if i > 1:
+                c_passes(order[i - 1][1], order[i - 1][0])
+        for k in range(K_PASSES):
+            shared(interleave_h, k, cut=2, end=4)
+            if k == 0:
+                quantise_b(3, 1)
+                c_passes(1, 3)
+                widen_theta()
+            else:
+                quantise_h(k - 1)
+        c_out(0, 0, on_scalar)
+        c_out(0, 2, on_vector)
+        quantise_h(2)
+        c_out(0, 1, on_scalar)
+        c_out(0, 3, on_vector)
+        for c in range(4):
+            v_passes(0, c)
+        interleave_c(0, 0, W, on_vector)
+        for t in range(3):
+            c_out(1, t, on_scalar)
+            v_out(0, t, on_scalar)
+        c_out(1, 3, on_vector)
+        v_out(0, 3, on_scalar)
+        quantise_c(0)
+        v_passes(1, 0)
+        v_passes(1, 1)
+        interleave_c(1, 0, W, on_vector)
+        quantise_v(0)
+        d_passes(0, 0)
+        v_out(1, 0, on_scalar)
+        v_out(1, 1, on_scalar)
+        quantise_c(1)
+
+        SPLIT = 352
+        def interleave_y_shared(g, half):
+            if SPLIT:
+                interleave_y(g, half, 0, SPLIT, on_gpsimd)
+            interleave_y(g, half, SPLIT, W, on_scalar)
+        last = len(order) - 1
+        for i, (g, half) in enumerate(order):
+            ahead = g + 1 + half
+            chunks = (2, 3) if half == 0 else (0, 1)
+            if i > 0:
+                interleave_y_shared(*order[i - 1])
+            for s in range(PACK):
+                y_out(g, half, s)
+                if i == last:
+                    store_y(g, half, s, s + 1)
+                elif s % 2:
+                    store_y(g, half, s - 1, s + 1)
+            if half == 1 and g + 1 < GROUPS:
+                quantise_v(g + 1)
+            if half == 0:
+                d_passes(g, 1)
+            if ahead < GROUPS:
+                for c in chunks:
+                    v_passes(ahead, c)
+                    v_out(ahead, c, on_scalar)
+            if half == 1 and g + 1 < GROUPS:
+                d_passes(g + 1, 0)
+            if i >= LAG:
+                quantise_y(*order[i - LAG])
+                store_codes(*order[i - LAG])
+        if LAG == 2:
+            quantise_y(3, 0)
+            store_codes(3, 0)
+        shared(interleave_y, 3, 1, cut=320)
+        quantise_y(3, 1)
+        store_codes(3, 1)
+        store_scales()

@@ -24,8 +24,6 @@ K_PASSES = K // W
 QUADRANTS = 4
 BANKS = 8
 CHUNK = 128
-Y_GROUPED_BUFS = 1
-LAG = 1
 
 
 def tile_oblique_block_deflation_k4_kernel(
@@ -74,7 +72,7 @@ def tile_oblique_block_deflation_k4_kernel(
         h_raw = [kept("h_raw%d" % k, [P, PACK, R], BF16) for k in range(K_PASSES)]
         h_codes = [kept("h_codes%d" % k, [P, R], U32) for k in range(K_PASSES)]
         h_planes = [kept("h_planes%d" % k, [P, R], U8) for k in range(K_PASSES)]
-        z_codes = [kept("z_codes%d" % g, [P, K_PASSES, W], U32) for g in range(GROUPS)]
+        z_codes = {}
         z_planes = kept("z_planes", [P, N], U8)
         l_raw = kept("l_raw", [P, GROUPS, 2 * R], U8)
         l_codes = kept("l_codes", [P, GROUPS, 2 * R], U8)
@@ -122,11 +120,14 @@ def tile_oblique_block_deflation_k4_kernel(
                 out=l_raw[:].bitcast(I32), in_=l_words.rearrange("g p n -> p g n").bitcast(I32)
             )
 
-        def load_z(g):
+        def load_z(g, lo=0, hi=4):
+            tile = kept("z_codes%d%d" % (g, lo), [P, K_PASSES, CHUNK * (hi - lo)], U32)
+            for c in range(lo, hi):
+                z_codes[g, c] = tile[:, :, CHUNK * (c - lo) : CHUNK * (c - lo + 1)]
             flat = z_words.rearrange("k p n t -> p k (n t)")
             nc.sync.dma_start(
-                out=z_codes[g][:].bitcast(I32),
-                in_=flat[:, :, PACK * W * g : PACK * W * (g + 1)].bitcast(I32),
+                out=tile[:].bitcast(I32),
+                in_=flat[:, :, PACK * (W * g + CHUNK * lo) : PACK * (W * g + CHUNK * hi)].bitcast(I32),
             )
 
         def load_l_scales():
@@ -146,13 +147,13 @@ def tile_oblique_block_deflation_k4_kernel(
         def load_theta():
             with nc.allow_non_contiguous_dma(reason="one theta value a slot"):
                 for i in range(4):
-                    nc.gpsimd.dma_start(
+                    nc.sync.dma_start(
                         out=theta_raw[i:P:4, :],
                         in_=theta.rearrange("(a t i) -> i a t", t=PACK, i=4)[i],
                     )
 
         def load_e():
-            nc.gpsimd.dma_start(out=e_cols[:], in_=e.rearrange("(g p t) -> p g t", p=P, t=PACK))
+            nc.sync.dma_start(out=e_cols[:], in_=e.rearrange("(g p t) -> p g t", p=P, t=PACK))
 
         def widen_theta():
             nc.vector.tensor_copy(out=theta_f32[:], in_=theta_raw[:])
@@ -225,7 +226,7 @@ def tile_oblique_block_deflation_k4_kernel(
             give_bank(("c", half, t))
 
         def interleave_c(half, lo, hi, copy):
-            interleave(copy, grouped_tile(("c", half), "grouped_c", 2), c_rows[half], lo, hi)
+            interleave(copy, grouped_tile(("c", half), "grouped_y_gpsimd", 1), c_rows[half], lo, hi)
 
         def quantise_c(half):
             quantise(("c", half), c_codes[half], c_planes[half][:])
@@ -238,7 +239,7 @@ def tile_oblique_block_deflation_k4_kernel(
                         out=bank[:, CHUNK * t : CHUNK * (t + 1)],
                         lhsT=h_codes[k][:, P * t : P * (t + 1)].bitcast(FP8X4),
                         lhsT_scale=h_planes[k][:, P * t : P * (t + 1)],
-                        rhs=z_codes[g][:, k, CHUNK * c : CHUNK * (c + 1)].bitcast(FP8X4),
+                        rhs=z_codes[g, c][:, k, :].bitcast(FP8X4),
                         rhs_scale=z_planes[4 * k : P, W * g + CHUNK * c : W * g + CHUNK * (c + 1)],
                         start=(k == 0),
                         stop=(k == K_PASSES - 1),
@@ -269,7 +270,7 @@ def tile_oblique_block_deflation_k4_kernel(
 
         def y_out(g, half, s):
             if s == 0:
-                y_rows[g, half] = staged("y_rows", [P, PACK, W], F32, 5)
+                y_rows[g, half] = staged("y_rows", [P, PACK, W], F32, 6)
             nc.vector.scalar_tensor_tensor(
                 out=y_rows[g, half][:, s, :],
                 in0=b_raw[g, half][:, s, :],
@@ -280,24 +281,33 @@ def tile_oblique_block_deflation_k4_kernel(
             )
             give_bank(("d", g, half, s))
 
-        def interleave_y(g, half, lo, hi, copy):
-            interleave(copy, grouped_tile(("y", g, half), "grouped_y", Y_GROUPED_BUFS), y_rows[g, half], lo, hi)
+        def interleave_y(g, piece, lo, hi, copy):
+            first, last = piece
+            key = ("y", g, piece)
+            if key not in grouped:
+                if copy is on_gpsimd:
+                    grouped[key] = staged("grouped_y_gpsimd", [P, last - first, PACK], BF16, 1)
+                else:
+                    grouped[key] = staged("grouped_y", [P, last - first, PACK], BF16, 3)
+            interleave(copy, grouped[key], y_rows[g, first // W], lo, hi)
 
-        def quantise_y(g, half):
-            y_codes[g, half] = staged("y_codes", [P, W], U32, 4)
-            quantise(("y", g, half), y_codes[g, half], y_planes[4 * g : P, cols(half)])
+        def quantise_y(g, piece):
+            first, last = piece
+            if g not in y_codes:
+                y_codes[g] = staged("y_codes", [P, M], U32, 2)
+            quantise(("y", g, piece), y_codes[g][:, first:last], y_planes[4 * g : P, first:last])
 
-        def store_y(g, half, lo, hi):
+        def store_y(g, lo, hi, first, last):
             nc.sync.dma_start(
-                out=out_0[rows(g), cols(half)].rearrange("(p s) m -> p s m", s=PACK)[:, lo:hi, :],
-                in_=y_rows[g, half][:, lo:hi, :],
+                out=out_0[rows(g), first:last].rearrange("(p s) m -> p s m", s=PACK)[:, lo:hi, :],
+                in_=y_rows[g, first // W][:, lo:hi, :],
             )
 
-        def store_codes(g, half):
+        def store_codes(g, first, last):
             flat = out_1[g].rearrange("p m t -> p (m t)")
             nc.sync.dma_start(
-                out=flat[:, PACK * W * half : PACK * W * (half + 1)].bitcast(I32),
-                in_=y_codes[g, half][:].bitcast(I32),
+                out=flat[:, PACK * first : PACK * last].bitcast(I32),
+                in_=y_codes[g][:, first:last].bitcast(I32),
             )
 
         def store_scales():
@@ -308,21 +318,24 @@ def tile_oblique_block_deflation_k4_kernel(
                 )
 
         clear_planes()
-        load_theta()
-        load_e()
         load_b(0, 0)
         load_b(0, 1)
         load_b(1, 0)
         load_l_scales()
         load_l()
         load_b(1, 1)
-        for u in [(2, 0), (2, 1), (3, 0), (3, 1)]:
-            load_b(*u)
-        load_h(0)
+        load_b(2, 0)
+        load_b(2, 1)
+        load_theta()
+        load_b(3, 0)
+        load_b(3, 1)
+        for k in range(K_PASSES):
+            load_h(k)
         load_z_scales()
-        load_h(1)
-        load_h(2)
-        for g in range(GROUPS):
+        load_z(0, 0, 2)
+        load_z(0, 2, 4)
+        load_e()
+        for g in range(1, GROUPS):
             load_z(g)
 
         MID = W // 2
@@ -338,25 +351,26 @@ def tile_oblique_block_deflation_k4_kernel(
                 step(*key, cut, end, on_scalar)
         order = [(g, half) for g in range(GROUPS) for half in range(HALVES)]
 
-        CUT = 240
+        CUT = 256
         for i, (g, half) in enumerate(order):
             interleave_b(g, half, 0, CUT, on_vector)
             interleave_b(g, half, CUT, W, on_scalar_by_activation if i == 0 else on_scalar)
-            if i > 0:
+            if 0 < i < 7:
                 quantise_b(*order[i - 1])
             if i == 2:
                 permute_l()
                 c_passes(0, 0)
-            if i > 1:
+            if 1 < i < 7:
                 c_passes(order[i - 1][1], order[i - 1][0])
         for k in range(K_PASSES):
             shared(interleave_h, k, cut=2, end=4)
-            if k == 0:
-                quantise_b(3, 1)
-                c_passes(1, 3)
-                widen_theta()
-            else:
+            if k > 0:
                 quantise_h(k - 1)
+            if k == 0:
+                widen_theta()
+            if k < 2:
+                quantise_b(3, k)
+                c_passes(k, 3)
         c_out(0, 0, on_scalar)
         c_out(0, 2, on_vector)
         quantise_h(2)
@@ -371,49 +385,47 @@ def tile_oblique_block_deflation_k4_kernel(
         c_out(1, 3, on_vector)
         v_out(0, 3, on_scalar)
         quantise_c(0)
-        v_passes(1, 0)
-        v_passes(1, 1)
+        def v_chunk(g, c):
+            if g < GROUPS:
+                v_passes(g, c)
+                v_out(g, c, on_scalar)
+        v_chunk(1, 0)
+        v_chunk(1, 1)
         interleave_c(1, 0, W, on_vector)
         quantise_v(0)
-        d_passes(0, 0)
-        v_out(1, 0, on_scalar)
-        v_out(1, 1, on_scalar)
         quantise_c(1)
-
-        SPLIT = 352
-        def interleave_y_shared(g, half):
-            if SPLIT:
-                interleave_y(g, half, 0, SPLIT, on_gpsimd)
-            interleave_y(g, half, SPLIT, W, on_scalar)
+        SPLIT = 320
+        def piece(half):
+            return (W * half, W * (half + 1))
+        def finish(g, half):
+            quantise_y(g, piece(half))
+            store_codes(g, *piece(half))
+        d_passes(0, 0)
         last = len(order) - 1
         for i, (g, half) in enumerate(order):
             ahead = g + 1 + half
             chunks = (2, 3) if half == 0 else (0, 1)
             if i > 0:
-                interleave_y_shared(*order[i - 1])
+                interleave_y(order[i - 1][0], piece(order[i - 1][1]), 0, SPLIT, on_gpsimd)
+                interleave_y(order[i - 1][0], piece(order[i - 1][1]), SPLIT, W, on_scalar)
             for s in range(PACK):
                 y_out(g, half, s)
                 if i == last:
-                    store_y(g, half, s, s + 1)
+                    store_y(g, s, s + 1, *piece(half))
                 elif s % 2:
-                    store_y(g, half, s - 1, s + 1)
+                    store_y(g, s - 1, s + 1, *piece(half))
             if half == 1 and g + 1 < GROUPS:
                 quantise_v(g + 1)
             if half == 0:
                 d_passes(g, 1)
-            if ahead < GROUPS:
-                for c in chunks:
-                    v_passes(ahead, c)
-                    v_out(ahead, c, on_scalar)
+            for c in chunks:
+                v_chunk(ahead, c)
             if half == 1 and g + 1 < GROUPS:
                 d_passes(g + 1, 0)
-            if i >= LAG:
-                quantise_y(*order[i - LAG])
-                store_codes(*order[i - LAG])
-        if LAG == 2:
-            quantise_y(3, 0)
-            store_codes(3, 0)
-        shared(interleave_y, 3, 1, cut=320)
-        quantise_y(3, 1)
-        store_codes(3, 1)
+            if 0 < i < last:
+                finish(*order[i - 1])
+        interleave_y(3, piece(1), 0, 320, on_vector)
+        interleave_y(3, piece(1), 320, W, on_scalar)
+        finish(3, 0)
+        finish(3, 1)
         store_scales()

@@ -73,7 +73,8 @@ def tile_oblique_block_deflation_k4_kernel(
         h_codes = [kept("h_codes%d" % k, [P, R], U32) for k in range(K_PASSES)]
         h_planes = [kept("h_planes%d" % k, [P, R], U8) for k in range(K_PASSES)]
         z_codes = {}
-        z_planes = kept("z_planes", [P, N], U8)
+        z_planes_first = kept("z_planes_first", [P, K_PASSES, W], U8)
+        z_planes_rest = kept("z_planes_rest", [P, K_PASSES, N - W], U8)
         l_raw = kept("l_raw", [P, GROUPS, 2 * R], U8)
         l_codes = kept("l_codes", [P, GROUPS, 2 * R], U8)
         l_planes_raw = kept("l_planes_raw", [P, GROUPS, R], U8)
@@ -84,7 +85,7 @@ def tile_oblique_block_deflation_k4_kernel(
         c_planes = [kept("c_planes%d" % half, [P, W], U8) for half in range(HALVES)]
         c_rows = [kept("c_rows%d" % half, [P, PACK, W], BF16) for half in range(HALVES)]
         y_planes = kept("y_planes", [P, M], U8)
-        theta_raw = kept("theta_raw", [P, PACK], BF16)
+        theta_raw = kept("theta_raw", [P, 13], BF16)
         theta_f32 = kept("theta_f32", [P, PACK], F32)
         e_cols = kept("e_cols", [P, GROUPS, PACK], BF16)
 
@@ -99,12 +100,20 @@ def tile_oblique_block_deflation_k4_kernel(
 
         def clear_planes():
             nc.vector.memset(l_planes_raw[:].rearrange("p g r -> p (g r)").bitcast(I32), 0)
-            nc.vector.memset(z_planes[:].bitcast(I32), 0)
+            nc.vector.memset(z_planes_first[:].rearrange("p k n -> p (k n)").bitcast(I32), 0)
+            nc.vector.memset(z_planes_rest[:].rearrange("p k n -> p (k n)").bitcast(I32), 0)
 
         def load_b(g, half):
             tile = kept("b_raw%d%d" % (g, half), [P, PACK, W], BF16)
             b_raw[g, half] = tile[:]
             nc.sync.dma_start(out=tile[:], in_=b[rows(g), cols(half)].rearrange("(p t) m -> p t m", t=PACK))
+
+        def load_b_first(cut):
+            tile = kept("b_raw00", [P, PACK, W], BF16)
+            b_raw[0, 0] = tile[:]
+            src = b[rows(0), cols(0)].rearrange("(p t) m -> p t m", t=PACK)
+            nc.sync.dma_start(out=tile[:, :, 0:cut], in_=src[:, :, 0:cut])
+            nc.sync.dma_start(out=tile[:, :, cut:W], in_=src[:, :, cut:W])
 
         def load_b_rows(g):
             tile = kept("b_rows%d" % g, [P, PACK, M], BF16)
@@ -137,26 +146,29 @@ def tile_oblique_block_deflation_k4_kernel(
                     in_=l_scales[:, 4 * q : 4 * q + 4, :].rearrange("g r n -> r g n").bitcast(I32),
                 )
 
-        def load_z_scales():
+        def load_z_scales(tile, first, last):
             for q in range(QUADRANTS):
                 nc.sync.dma_start(
-                    out=z_planes[32 * q : 32 * q + 4 * K_PASSES, :].bitcast(I32),
-                    in_=z_scales[:, 4 * q : 4 * q + 4, :].bitcast(I32),
+                    out=tile[32 * q : 32 * q + 4, :, :].bitcast(I32),
+                    in_=z_scales[:, 4 * q : 4 * q + 4, first:last].rearrange("k r n -> r k n").bitcast(I32),
                 )
 
+        def z_plane(g, k, c):
+            if g == 0:
+                return z_planes_first[:, k, CHUNK * c : CHUNK * (c + 1)]
+            return z_planes_rest[:, k, W * (g - 1) + CHUNK * c : W * (g - 1) + CHUNK * (c + 1)]
+
         def load_theta():
-            with nc.allow_non_contiguous_dma(reason="one theta value a slot"):
-                for i in range(4):
-                    nc.sync.dma_start(
-                        out=theta_raw[i:P:4, :],
-                        in_=theta.rearrange("(a t i) -> i a t", t=PACK, i=4)[i],
-                    )
+            for i in range(4):
+                nc.sync.dma_start(
+                    out=theta_raw[i:P:4, :], in_=theta.rearrange("(a x) -> a x", x=16)[:, i : i + 13]
+                )
 
         def load_e():
             nc.sync.dma_start(out=e_cols[:], in_=e.rearrange("(g p t) -> p g t", p=P, t=PACK))
 
         def widen_theta():
-            nc.vector.tensor_copy(out=theta_f32[:], in_=theta_raw[:])
+            nc.vector.tensor_copy(out=theta_f32[:], in_=theta_raw[:, 0:13:4])
 
         def grouped_tile(key, tag, bufs):
             if key not in grouped:
@@ -164,6 +176,9 @@ def tile_oblique_block_deflation_k4_kernel(
             return grouped[key]
 
         def interleave(copy, dst, src, lo, hi):
+            if copy is on_gpsimd:
+                copy(out=dst[:, lo:hi, :], in_=src[:, :, lo:hi].rearrange("p t c -> p c t"))
+                return
             copy(
                 out=dst[:, lo:hi, :].rearrange("p (c i) t -> p c t i", i=4),
                 in_=src[:, :, lo:hi].rearrange("p t (c i) -> p c t i", i=4),
@@ -226,7 +241,7 @@ def tile_oblique_block_deflation_k4_kernel(
             give_bank(("c", half, t))
 
         def interleave_c(half, lo, hi, copy):
-            interleave(copy, grouped_tile(("c", half), "grouped_y_gpsimd", 1), c_rows[half], lo, hi)
+            interleave(copy, grouped_tile(("c", half), *(("grouped_y", 3), ("grouped_y_gpsimd", 1))[half]), c_rows[half], lo, hi)
 
         def quantise_c(half):
             quantise(("c", half), c_codes[half], c_planes[half][:])
@@ -240,7 +255,7 @@ def tile_oblique_block_deflation_k4_kernel(
                         lhsT=h_codes[k][:, P * t : P * (t + 1)].bitcast(FP8X4),
                         lhsT_scale=h_planes[k][:, P * t : P * (t + 1)],
                         rhs=z_codes[g, c][:, k, :].bitcast(FP8X4),
-                        rhs_scale=z_planes[4 * k : P, W * g + CHUNK * c : W * g + CHUNK * (c + 1)],
+                        rhs_scale=z_plane(g, k, c),
                         start=(k == 0),
                         stop=(k == K_PASSES - 1),
                     )
@@ -329,14 +344,17 @@ def tile_oblique_block_deflation_k4_kernel(
         load_theta()
         load_b(3, 0)
         load_b(3, 1)
-        for k in range(K_PASSES):
-            load_h(k)
-        load_z_scales()
+        load_h(0)
+        load_h(1)
+        load_h(2)
+        load_z_scales(z_planes_first, 0, W)
         load_z(0, 0, 2)
         load_z(0, 2, 4)
+        load_z(1)
+        load_z_scales(z_planes_rest, W, N)
         load_e()
-        for g in range(1, GROUPS):
-            load_z(g)
+        load_z(2)
+        load_z(3)
 
         MID = W // 2
         def c_passes(half, g):
@@ -355,46 +373,45 @@ def tile_oblique_block_deflation_k4_kernel(
         for i, (g, half) in enumerate(order):
             interleave_b(g, half, 0, CUT, on_vector)
             interleave_b(g, half, CUT, W, on_scalar_by_activation if i == 0 else on_scalar)
-            if 0 < i < 7:
+            if i > 0:
                 quantise_b(*order[i - 1])
             if i == 2:
                 permute_l()
                 c_passes(0, 0)
-            if 1 < i < 7:
+            if i > 1:
                 c_passes(order[i - 1][1], order[i - 1][0])
         for k in range(K_PASSES):
             shared(interleave_h, k, cut=2, end=4)
             if k > 0:
                 quantise_h(k - 1)
             if k == 0:
+                quantise_b(3, 1)
+                c_passes(1, 3)
                 widen_theta()
-            if k < 2:
-                quantise_b(3, k)
-                c_passes(k, 3)
+        quantise_h(2)
         c_out(0, 0, on_scalar)
         c_out(0, 2, on_vector)
-        quantise_h(2)
-        c_out(0, 1, on_scalar)
         c_out(0, 3, on_vector)
+        c_out(0, 1, on_scalar)
         for c in range(4):
             v_passes(0, c)
+        c_out(1, 3, on_vector)
         interleave_c(0, 0, W, on_vector)
         for t in range(3):
             c_out(1, t, on_scalar)
             v_out(0, t, on_scalar)
-        c_out(1, 3, on_vector)
         v_out(0, 3, on_scalar)
-        quantise_c(0)
         def v_chunk(g, c):
             if g < GROUPS:
                 v_passes(g, c)
                 v_out(g, c, on_scalar)
         v_chunk(1, 0)
         v_chunk(1, 1)
+        quantise_c(0)
         interleave_c(1, 0, W, on_vector)
         quantise_v(0)
         quantise_c(1)
-        SPLIT = 320
+        SPLIT = 256
         def piece(half):
             return (W * half, W * (half + 1))
         def finish(g, half):

from contextlib import ExitStack

import concourse.mybir as mybir

N, M, K, R = 2048, 1024, 1536, 512
FLOPS = 2 * K * N * R + 2 * N * R * M + 2 * R * N * M

F32 = mybir.dt.float32
BF16 = mybir.dt.bfloat16
I32 = mybir.dt.int32
U32 = mybir.dt.uint32
U8 = mybir.dt.uint8
FP8X4 = mybir.dt.float8_e4m3fn_x4
FP4X4 = mybir.dt.float4_e2m1fn_x4
COPY = mybir.ActivationFunctionType.Copy
ALU = mybir.AluOpType

P = 128
PACK = 4
W = 512
GROUPS = N // W
HALVES = M // W
K_PASSES = K // W
QUADRANTS = 4
BANKS = 8
CHUNK = 128


def tile_oblique_block_deflation_k4_kernel(
    tc, z_words, z_scales, h, l_words, l_scales, b, theta, e, out_0, out_1, out_2
):
    nc = tc.nc
    with ExitStack() as ctx:
        keep = ctx.enter_context(tc.tile_pool(name="keep", bufs=1))
        stage = ctx.enter_context(tc.tile_pool(name="stage", bufs=1))
        psum = ctx.enter_context(tc.psum_pool(name="psum", bufs=1))
        ctx.enter_context(tc.manual_schedule())

        def kept(name, shape, dtype):
            return keep.tile(shape, dtype, name=name, align_bytes=64)

        def staged(tag, shape, dtype, bufs):
            return stage.tile(shape, dtype, name=tag, tag=tag, bufs=bufs, align_bytes=64)

        free_banks = list(range(BANKS))
        banks = {}
        bank_number = {}

        def take_bank(key):
            bank_number[key] = free_banks.pop(0)
            tag = "bank%d" % bank_number[key]
            banks[key] = psum.tile([P, W], F32, name=tag, tag=tag)
            return banks[key]

        def give_bank(key):
            free_banks.append(bank_number[key])

        on_vector = nc.vector.tensor_copy
        on_scalar = nc.scalar.copy

        def on_scalar_by_activation(out, in_):
            nc.scalar.activation(out=out, in_=in_, func=COPY)

        def on_gpsimd(out, in_):
            nc.gpsimd.tensor_scalar(out=out, in0=in_, scalar1=1.0, scalar2=0.0, op0=ALU.mult, op1=ALU.add)

        units = [(g, half) for g in range(GROUPS) for half in range(HALVES)]
        b_raw = {}
        b_codes = {u: kept("b_codes%d%d" % u, [P, W], U32) for u in units}
        b_planes = {u: kept("b_planes%d%d" % u, [P, W], U8) for u in units}
        y_codes = {}
        h_raw = [kept("h_raw%d" % k, [P, PACK, R], BF16) for k in range(K_PASSES)]
        h_codes = [kept("h_codes%d" % k, [P, R], U32) for k in range(K_PASSES)]
        h_planes = [kept("h_planes%d" % k, [P, R], U8) for k in range(K_PASSES)]
        z_codes = {}
        z_planes_first = kept("z_planes_first", [P, K_PASSES, W], U8)
        z_planes_rest = kept("z_planes_rest", [P, K_PASSES, N - W], U8)
        l_raw = kept("l_raw", [P, GROUPS, 2 * R], U8)
        l_codes = kept("l_codes", [P, GROUPS, 2 * R], U8)
        l_planes_raw = kept("l_planes_raw", [P, GROUPS, R], U8)
        l_planes = kept("l_planes", [P, GROUPS, R], U8)
        v_codes = [kept("v_codes%d" % g, [P, W], U32) for g in range(GROUPS)]
        v_planes = [kept("v_planes%d" % g, [P, W], U8) for g in range(GROUPS)]
        c_codes = [kept("c_codes%d" % half, [P, W], U32) for half in range(HALVES)]
        c_planes = [kept("c_planes%d" % half, [P, W], U8) for half in range(HALVES)]
        c_rows = [kept("c_rows%d" % half, [P, PACK, W], BF16) for half in range(HALVES)]
        y_planes = kept("y_planes", [P, M], U8)
        theta_raw = kept("theta_raw", [P, 13], BF16)
        theta_f32 = kept("theta_f32", [P, PACK], F32)
        e_cols = kept("e_cols", [P, GROUPS, PACK], BF16)

        grouped = {}
        y_rows = {}

        def cols(half):
            return slice(half * W, (half + 1) * W)

        def rows(g):
            return slice(g * W, (g + 1) * W)

        def clear_planes():
            nc.vector.memset(l_planes_raw[:].rearrange("p g r -> p (g r)").bitcast(I32), 0)
            nc.vector.memset(z_planes_first[:].rearrange("p k n -> p (k n)").bitcast(I32), 0)
            nc.vector.memset(z_planes_rest[:].rearrange("p k n -> p (k n)").bitcast(I32), 0)

        def load_b(g, half):
            tile = kept("b_raw%d%d" % (g, half), [P, PACK, W], BF16)
            b_raw[g, half] = tile[:]
            nc.sync.dma_start(out=tile[:], in_=b[rows(g), cols(half)].rearrange("(p t) m -> p t m", t=PACK))

        def load_b_first(cut):
            tile = kept("b_raw00", [P, PACK, W], BF16)
            b_raw[0, 0] = tile[:]
            src = b[rows(0), cols(0)].rearrange("(p t) m -> p t m", t=PACK)
            nc.sync.dma_start(out=tile[:, :, 0:cut], in_=src[:, :, 0:cut])
            nc.sync.dma_start(out=tile[:, :, cut:W], in_=src[:, :, cut:W])

        def load_b_rows(g):
            tile = kept("b_rows%d" % g, [P, PACK, M], BF16)
            for half in range(HALVES):
                b_raw[g, half] = tile[:, :, cols(half)]
            nc.sync.dma_start(out=tile[:], in_=b[rows(g), :].rearrange("(p t) m -> p t m", t=PACK))

        def load_h(k):
            nc.sync.dma_start(out=h_raw[k][:], in_=h[rows(k), :].rearrange("(p t) r -> p t r", t=PACK))

        def load_l():
            nc.sync.dma_start(
                out=l_raw[:].bitcast(I32), in_=l_words.rearrange("g p n -> p g n").bitcast(I32)
            )

        def load_z(g, lo=0, hi=4):
            tile = kept("z_codes%d%d" % (g, lo), [P, K_PASSES, CHUNK * (hi - lo)], U32)
            for c in range(lo, hi):
                z_codes[g, c] = tile[:, :, CHUNK * (c - lo) : CHUNK * (c - lo + 1)]
            flat = z_words.rearrange("k p n t -> p k (n t)")
            nc.sync.dma_start(
                out=tile[:].bitcast(I32),
                in_=flat[:, :, PACK * (W * g + CHUNK * lo) : PACK * (W * g + CHUNK * hi)].bitcast(I32),
            )

        def load_l_scales():
            for q in range(QUADRANTS):
                nc.sync.dma_start(
                    out=l_planes_raw[32 * q : 32 * q + 4, :, :].bitcast(I32),
                    in_=l_scales[:, 4 * q : 4 * q + 4, :].rearrange("g r n -> r g n").bitcast(I32),
                )

        def load_z_scales(tile, first, last):
            for q in range(QUADRANTS):
                nc.sync.dma_start(
                    out=tile[32 * q : 32 * q + 4, :, :].bitcast(I32),
                    in_=z_scales[:, 4 * q : 4 * q + 4, first:last].rearrange("k r n -> r k n").bitcast(I32),
                )

        def z_plane(g, k, c):
            if g == 0:
                return z_planes_first[:, k, CHUNK * c : CHUNK * (c + 1)]
            return z_planes_rest[:, k, W * (g - 1) + CHUNK * c : W * (g - 1) + CHUNK * (c + 1)]

        def load_theta():
            for i in range(4):
                nc.sync.dma_start(
                    out=theta_raw[i:P:4, :], in_=theta.rearrange("(a x) -> a x", x=16)[:, i : i + 13]
                )

        def load_e():
            nc.sync.dma_start(out=e_cols[:], in_=e.rearrange("(g p t) -> p g t", p=P, t=PACK))

        def widen_theta():
            nc.vector.tensor_copy(out=theta_f32[:], in_=theta_raw[:, 0:13:4])

        def grouped_tile(key, tag, bufs):
            if key not in grouped:
                grouped[key] = staged(tag, [P, W, PACK], BF16, bufs)
            return grouped[key]

        def interleave(copy, dst, src, lo, hi):
            if copy is on_gpsimd:
                copy(out=dst[:, lo:hi, :], in_=src[:, :, lo:hi].rearrange("p t c -> p c t"))
                return
            copy(
                out=dst[:, lo:hi, :].rearrange("p (c i) t -> p c t i", i=4),
                in_=src[:, :, lo:hi].rearrange("p t (c i) -> p c t i", i=4),
            )

        def quantise(key, codes, plane):
            nc.vector.quantize_mx(
                out=codes[:].bitcast(FP8X4), scales=plane, in_=grouped[key][:].rearrange("p w t -> p (w t)")
            )

        def interleave_b(g, half, lo, hi, copy):
            interleave(copy, grouped_tile(("b", g, half), "grouped_in", 4), b_raw[g, half], lo, hi)

        def quantise_b(g, half):
            quantise(("b", g, half), b_codes[g, half], b_planes[g, half][:])

        def interleave_h(k, lo, hi, copy):
            dst = grouped_tile(("h", k), "grouped_in", 4)
            copy(
                out=dst[:].rearrange("p (t a i) j -> p a t j i", t=PACK, i=4)[:, :, lo:hi],
                in_=h_raw[k][:].rearrange("p j (a t i) -> p a t j i", t=PACK, i=4)[:, :, lo:hi],
            )

        def quantise_h(k):
            quantise(("h", k), h_codes[k], h_planes[k][:])

        def permute_l():
            nc.vector.tensor_copy(
                out=l_codes[:].bitcast(I32).rearrange("p g (t a w) -> p g t a w", t=PACK, w=2),
                in_=l_raw[:].bitcast(I32).rearrange("p g (a t w) -> p g t a w", t=PACK, w=2),
            )
            nc.vector.tensor_copy(
                out=l_planes[:].bitcast(I32).rearrange("p g (t a) -> p g t a", t=PACK),
                in_=l_planes_raw[:].bitcast(I32).rearrange("p g (a t) -> p g t a", t=PACK),
            )

        def c_pass(half, t, g):
            if g == 0:
                take_bank(("c", half, t))
            nc.tensor.matmul_mx(
                out=banks["c", half, t][:],
                lhsT=l_codes[:, g, 2 * P * t : 2 * P * (t + 1)].bitcast(FP4X4),
                lhsT_scale=l_planes[:, g, P * t : P * (t + 1)],
                rhs=b_codes[g, half][:].bitcast(FP8X4),
                rhs_scale=b_planes[g, half][:],
                start=(g == 0),
                stop=(g == GROUPS - 1),
            )

        def c_out(half, t, copy):
            if copy is on_vector:
                nc.vector.tensor_scalar(
                    out=c_rows[half][:, t, :], in0=banks["c", half, t][:], scalar1=theta_f32[:, t : t + 1],
                    scalar2=None, op0=ALU.mult,
                )
            else:
                nc.scalar.activation(
                    out=c_rows[half][:, t, :], in_=banks["c", half, t][:], func=COPY, scale=theta_f32[:, t : t + 1]
                )
            give_bank(("c", half, t))

        def interleave_c(half, lo, hi, copy):
            interleave(copy, grouped_tile(("c", half), *(("grouped_y", 3), ("grouped_y_gpsimd", 1))[half]), c_rows[half], lo, hi)

        def quantise_c(half):
            quantise(("c", half), c_codes[half], c_planes[half][:])

        def v_passes(g, c):
            bank = take_bank(("v", g, c))
            for t in range(PACK):
                for k in range(K_PASSES):
                    nc.tensor.matmul_mx(
                        out=bank[:, CHUNK * t : CHUNK * (t + 1)],
                        lhsT=h_codes[k][:, P * t : P * (t + 1)].bitcast(FP8X4),
                        lhsT_scale=h_planes[k][:, P * t : P * (t + 1)],
                        rhs=z_codes[g, c][:, k, :].bitcast(FP8X4),
                        rhs_scale=z_plane(g, k, c),
                        start=(k == 0),
                        stop=(k == K_PASSES - 1),
                    )

        def v_out(g, c, copy):
            dst = grouped_tile(("v", g), "grouped_v", 2)
            copy(
                out=dst[:].rearrange("p (s m) t -> p s m t", s=PACK)[:, :, 32 * c : 32 * (c + 1), :],
                in_=banks["v", g, c][:].rearrange("p (t m s) -> p s m t", t=PACK, s=PACK),
            )
            give_bank(("v", g, c))

        def quantise_v(g):
            quantise(("v", g), v_codes[g], v_planes[g][:])

        def d_pass(g, half, s):
            take_bank(("d", g, half, s))
            nc.tensor.matmul_mx(
                out=banks["d", g, half, s][:],
                lhsT=v_codes[g][:, P * s : P * (s + 1)].bitcast(FP8X4),
                lhsT_scale=v_planes[g][:, P * s : P * (s + 1)],
                rhs=c_codes[half][:].bitcast(FP8X4),
                rhs_scale=c_planes[half][:],
                start=True,
                stop=True,
            )

        def y_out(g, half, s):
            if s == 0:
                y_rows[g, half] = staged("y_rows", [P, PACK, W], F32, 6)
            nc.vector.scalar_tensor_tensor(
                out=y_rows[g, half][:, s, :],
                in0=b_raw[g, half][:, s, :],
                scalar=e_cols[:, g, s : s + 1],
                in1=banks["d", g, half, s][:],
                op0=ALU.mult,
                op1=ALU.subtract,
            )
            give_bank(("d", g, half, s))

        def interleave_y(g, piece, lo, hi, copy):
            first, last = piece
            key = ("y", g, piece)
            if key not in grouped:
                if copy is on_gpsimd:
                    grouped[key] = staged("grouped_y_gpsimd", [P, last - first, PACK], BF16, 1)
                else:
                    grouped[key] = staged("grouped_y", [P, last - first, PACK], BF16, 3)
            interleave(copy, grouped[key], y_rows[g, first // W], lo, hi)

        def quantise_y(g, piece):
            first, last = piece
            if g not in y_codes:
                y_codes[g] = staged("y_codes", [P, M], U32, 2)
            quantise(("y", g, piece), y_codes[g][:, first:last], y_planes[4 * g : P, first:last])

        def store_y(g, lo, hi, first, last):
            nc.sync.dma_start(
                out=out_0[rows(g), first:last].rearrange("(p s) m -> p s m", s=PACK)[:, lo:hi, :],
                in_=y_rows[g, first // W][:, lo:hi, :],
            )

        def store_codes(g, first, last):
            flat = out_1[g].rearrange("p m t -> p (m t)")
            nc.sync.dma_start(
                out=flat[:, PACK * first : PACK * last].bitcast(I32),
                in_=y_codes[g][:, first:last].bitcast(I32),
            )

        def store_scales():
            for q in range(QUADRANTS):
                nc.scalar.dma_start(
                    out=out_2[:, 4 * q : 4 * q + 4, :].bitcast(I32),
                    in_=y_planes[32 * q : 32 * q + 4 * GROUPS, :].bitcast(I32),
                )

        clear_planes()
        load_b(0, 0)
        load_b(0, 1)
        load_b(1, 0)
        load_l_scales()
        load_l()
        load_b(1, 1)
        load_b(2, 0)
        load_b(2, 1)
        load_theta()
        load_b(3, 0)
        load_b(3, 1)
        load_h(0)
        load_h(1)
        load_h(2)
        load_z_scales(z_planes_first, 0, W)
        load_z(0, 0, 2)
        load_z(0, 2, 4)
        load_z(1)
        load_z_scales(z_planes_rest, W, N)
        load_e()
        load_z(2)
        load_z(3)

        MID = W // 2
        def c_passes(half, g):
            for t in range(PACK):
                c_pass(half, t, g)
        def d_passes(g, half):
            for s in range(PACK):
                d_pass(g, half, s)
        def shared(step, *key, cut=MID, end=W):
            step(*key, 0, cut, on_vector)
            if cut < end:
                step(*key, cut, end, on_scalar)
        order = [(g, half) for g in range(GROUPS) for half in range(HALVES)]

        CUT = 256
        for i, (g, half) in enumerate(order):
            interleave_b(g, half, 0, CUT, on_vector)
            interleave_b(g, half, CUT, W, on_scalar_by_activation if i == 0 else on_scalar)
            if i > 0:
                quantise_b(*order[i - 1])
            if i == 2:
                permute_l()
                c_passes(0, 0)
            if i > 1:
                c_passes(order[i - 1][1], order[i - 1][0])
        for k in range(K_PASSES):
            shared(interleave_h, k, cut=2, end=4)
            if k > 0:
                quantise_h(k - 1)
            if k == 0:
                quantise_b(3, 1)
                c_passes(1, 3)
                widen_theta()
        quantise_h(2)
        c_out(0, 0, on_scalar)
        c_out(0, 2, on_vector)
        c_out(0, 3, on_vector)
        c_out(0, 1, on_scalar)
        for c in range(4):
            v_passes(0, c)
        c_out(1, 3, on_vector)
        interleave_c(0, 0, W, on_vector)
        for t in range(3):
            c_out(1, t, on_scalar)
            v_out(0, t, on_scalar)
        v_out(0, 3, on_scalar)
        def v_chunk(g, c):
            if g < GROUPS:
                v_passes(g, c)
                v_out(g, c, on_scalar)
        v_chunk(1, 0)
        v_chunk(1, 1)
        quantise_c(0)
        interleave_c(1, 0, W, on_vector)
        quantise_v(0)
        quantise_c(1)
        SPLIT = 256
        def piece(half):
            return (W * half, W * (half + 1))
        def finish(g, half):
            quantise_y(g, piece(half))
            store_codes(g, *piece(half))
        d_passes(0, 0)
        last = len(order) - 1
        for i, (g, half) in enumerate(order):
            ahead = g + 1 + half
            chunks = (2, 3) if half == 0 else (0, 1)
            if i > 0:
                interleave_y(order[i - 1][0], piece(order[i - 1][1]), 0, SPLIT, on_gpsimd)
                interleave_y(order[i - 1][0], piece(order[i - 1][1]), SPLIT, W, on_scalar)
            for s in range(PACK):
                y_out(g, half, s)
                if i == last:
                    store_y(g, s, s + 1, *piece(half))
                elif s % 2:
                    store_y(g, s - 1, s + 1, *piece(half))
            if half == 1 and g + 1 < GROUPS:
                quantise_v(g + 1)
            if half == 0:
                d_passes(g, 1)
            for c in chunks:
                v_chunk(ahead, c)
            if half == 1 and g + 1 < GROUPS:
                d_passes(g + 1, 0)
            if 0 < i < last:
                finish(*order[i - 1])
        interleave_y(3, piece(1), 0, 320, on_vector)
        interleave_y(3, piece(1), 320, W, on_scalar)
        finish(3, 0)
        finish(3, 1)
        store_scales()
